import numpy as np
import ml_dtypes


def mxq(x, axis, fmt="e4m3"):
    dtype, down = {"e4m3": (ml_dtypes.float8_e4m3fn, 7), "e5m2": (ml_dtypes.float8_e5m2, 14)}[fmt]
    v = np.moveaxis(np.asarray(x, np.float32).astype(ml_dtypes.bfloat16).astype(np.float64), axis, -1)
    blocks = v.reshape(v.shape[:-1] + (-1, 32))
    amax = np.abs(blocks).max(-1, keepdims=True)
    byte = np.maximum(np.where(amax > 0, np.frexp(amax)[1] - 1 + 127, 0) - down, 1)
    scale = np.exp2(byte - 127.0)
    codes = (blocks / scale).astype(np.float32).astype(dtype).astype(np.float64)
    return np.moveaxis((codes * scale).reshape(v.shape), -1, axis)


WIDE = False


def mx_kscale(k, group=512):
    if not WIDE:
        return np.ones(k)
    levels = np.array([18, -18])
    if group != 512:
        return np.exp2(np.random.permutation(np.resize(levels, k // group))).repeat(group)
    if k % 512:
        return np.exp2(np.random.permutation(np.resize(levels, k // 32))).repeat(32)
    a = np.empty((k // 512, 16))
    for p in range(k // 512):
        a[p, :8] = np.random.permutation(np.resize(levels, 8))
        for g in range(8):
            far = levels[np.abs(levels - a[p, g]) >= 10]
            a[p, g + 8] = far[np.random.randint(len(far))]
    return np.exp2(a.ravel()).repeat(32)


def f64(x):
    return np.asarray(x).astype(np.float64)


G, D, M, N = 4, 128, 128, 512


def setup_inputs():
    n = np.random.standard_normal
    s = mx_kscale(D, 0)[:, None]
    return {
        "x": (n((G, D, N)) * s).astype(np.float32),
        "w": (n((G, D, M)) / np.sqrt(D) / s).astype(np.float32),
        "u": (n((G, D, M)) / np.sqrt(D) / s).astype(np.float32),
        "r": n((G, M, N)).astype(np.float32),
    }


def reference(x, w, u, r):
    xq = mxq(f64(x), 1, "e4m3")
    h = mxq(f64(w), 1, "e4m3").transpose(0, 2, 1) @ xq
    g = mxq(f64(u), 1, "e4m3").transpose(0, 2, 1) @ xq
    y = 1.0 / (1.0 + np.exp(-(h))) * g
    y = y + f64(r)
    return y

@@ -1,0 +1,214 @@
+from contextlib import ExitStack
+
+import concourse.mybir as mybir
+
+G, D, M, N = 4, 128, 128, 512
+FLOPS = 2 * 2 * G * D * M * N
+
+F32 = mybir.dt.float32
+BF16 = mybir.dt.bfloat16
+U32 = mybir.dt.uint32
+U8 = mybir.dt.uint8
+FP8X4 = mybir.dt.float8_e4m3fn_x4
+ACT = mybir.ActivationFunctionType
+ALU = mybir.AluOpType
+
+P = 128
+PACK = 4
+ROWS = 32
+NT = 128
+
+PROGRAM = [
+    ("warm",),
+    ("ld", "y", "w", 0, 128),
+    ("ld", "y", "x", 0, 128),
+    ("ld", "y", "u", 0, 128),
+    ("ld", "y", "x", 128, 256),
+    ("ld", "y", "x", 256, 384),
+    ("ld", "y", "x", 384, 512),
+    ("ldr", "y", 0, 4, 0, 256),
+    ("ldr", "y", 0, 4, 256, 512),
+    ("cast", "s", "w", 0, 128),
+    ("cast", "v", "x", 0, 128),
+    ("q", "w", 0, 128),
+    ("q", "x", 0, 128),
+    ("mm", "w", 0, 0),
+    ("mm", "w", 1, 0),
+    ("mm", "w", 2, 0),
+    ("mm", "w", 3, 0),
+    ("cast", "v", "u", 0, 64),
+    ("cast", "s", "u", 64, 128),
+    ("q", "u", 0, 128),
+    ("mm", "u", 0, 0),
+    ("mm", "u", 1, 0),
+    ("mm", "u", 2, 0),
+    ("mm", "u", 3, 0),
+    ("cast", "v", "x", 128, 256),
+    ("q", "x", 128, 256),
+    ("sig", 0, 0, 128),
+    ("mm", "w", 0, 128),
+    ("sig", 1, 0, 128),
+    ("mm", "w", 1, 128),
+    ("sig", 2, 0, 128),
+    ("mm", "w", 2, 128),
+    ("sig", 3, 0, 128),
+    ("mm", "w", 3, 128),
+    ("mul", 0, 0, 128),
+    ("mm", "u", 0, 128),
+    ("mul", 1, 0, 128),
+    ("mm", "u", 1, 128),
+    ("mul", 2, 0, 128),
+    ("mm", "u", 2, 128),
+    ("mul", 3, 0, 128),
+    ("mm", "u", 3, 128),
+    ("cast", "s", "x", 256, 384),
+    ("q", "x", 256, 384),
+    ("sig", 0, 128, 256),
+    ("mm", "w", 0, 256),
+    ("sig", 1, 128, 256),
+    ("mm", "w", 1, 256),
+    ("sig", 2, 128, 256),
+    ("mm", "w", 2, 256),
+    ("sig", 3, 128, 256),
+    ("mm", "w", 3, 256),
+    ("mul", 0, 128, 256),
+    ("mm", "u", 0, 256),
+    ("mul", 1, 128, 256),
+    ("mm", "u", 1, 256),
+    ("mul", 2, 128, 256),
+    ("mm", "u", 2, 256),
+    ("mul", 3, 128, 256),
+    ("mm", "u", 3, 256),
+    ("cast", "s", "x", 384, 512),
+    ("add", "v", 0, 1, 0, 256),
+    ("add", "v", 1, 2, 0, 256),
+    ("st", "y", 0, 2, 0, 256),
+    ("q", "x", 384, 512),
+    ("sig", 0, 256, 384),
+    ("mm", "w", 0, 384),
+    ("sig", 1, 256, 384),
+    ("mm", "w", 1, 384),
+    ("sig", 2, 256, 384),
+    ("mm", "w", 2, 384),
+    ("sig", 3, 256, 384),
+    ("mm", "w", 3, 384),
+    ("add", "v", 2, 3, 0, 256),
+    ("mul", 0, 256, 384),
+    ("mm", "u", 0, 384),
+    ("mul", 1, 256, 384),
+    ("mm", "u", 1, 384),
+    ("mul", 2, 256, 384),
+    ("mm", "u", 2, 384),
+    ("mul", 3, 256, 384),
+    ("mm", "u", 3, 384),
+    ("add", "v", 3, 4, 0, 256),
+    ("st", "y", 2, 4, 0, 256),
+    ("sig", 0, 384, 512),
+    ("sig", 1, 384, 512),
+    ("sig", 2, 384, 512),
+    ("sig", 3, 384, 512),
+    ("mul", 0, 384, 512),
+    ("mul", 1, 384, 512),
+    ("add", "v", 0, 1, 256, 512),
+    ("st", "y", 0, 1, 256, 512),
+    ("mul", 2, 384, 512),
+    ("add", "v", 1, 2, 256, 512),
+    ("st", "y", 1, 2, 256, 512),
+    ("mul", 3, 384, 512),
+    ("add", "v", 2, 3, 256, 512),
+    ("st", "y", 2, 3, 256, 512),
+    ("add", "v", 3, 4, 256, 512),
+    ("st", "y", 3, 4, 256, 512),
+]
+
+
+def tile_rows_gglu_sigmoid_res_kernel(tc, x, w, u, r, out):
+    nc = tc.nc
+    src = {
+        "x": x.rearrange("g (p j) n -> (g p) j n", j=PACK),
+        "w": w.rearrange("g (p j) m -> (g p) j m", j=PACK),
+        "u": u.rearrange("g (p j) m -> (g p) j m", j=PACK),
+    }
+    r_rows = r.rearrange("g m n -> m g n")
+    out_rows = out.rearrange("g m n -> m g n")
+    eng = {"v": nc.vector, "s": nc.scalar, "p": nc.gpsimd, "y": nc.sync}
+
+    with ExitStack() as ctx:
+        sb = ctx.enter_context(tc.tile_pool(name="sb", bufs=1))
+        ps = ctx.enter_context(tc.psum_pool(name="ps", bufs=1))
+        raw, grouped, codes, scales = {}, {}, {}, {}
+        for op in PROGRAM:
+            if op[0] == "ld":
+                raw[(op[2], op[3], op[4])] = sb.tile(
+                    [P, PACK, op[4] - op[3]], F32, name="raw_%s_%d" % (op[2], op[3]), align_bytes=64
+                )
+        for key, wd in (("w", M), ("u", M), ("x", N)):
+            grouped[key] = sb.tile([P, wd, PACK], BF16, name="grp_%s" % key, align_bytes=64)
+            codes[key] = sb.tile([P, wd], U32, name="codes_%s" % key, align_bytes=64)
+            scales[key] = sb.tile([P, wd], U8, name="scales_%s" % key, align_bytes=64)
+        banks = {}
+        for g in range(G):
+            for which in ("w", "u"):
+                banks[(g, which)] = ps.tile([P, N], F32, name="bank_%d_%s" % (g, which))
+        gate = sb.tile([P, G, N], F32, name="gate", align_bytes=64)
+        prod = sb.tile([P, G, N], F32, name="prod", align_bytes=64)
+        res = sb.tile([P, G, N], F32, name="res", align_bytes=64)
+        y = sb.tile([P, G, N], F32, name="y", align_bytes=64)
+        warm = sb.tile([P, 8], F32, name="warm", align_bytes=64)
+        warm_out = sb.tile([P, 8], F32, name="warm_out", align_bytes=64)
+
+        ctx.enter_context(tc.manual_schedule())
+        for op in PROGRAM:
+            kind = op[0]
+            if kind == "warm":
+                nc.gpsimd.memset(warm[:], 0.0)
+                nc.scalar.activation(out=warm_out[:], in_=warm[:], func=ACT.Sigmoid)
+            elif kind == "ld":
+                e, key, a, b = op[1:]
+                eng[e].dma_start(out=raw[(key, a, b)][:], in_=src[key][:, :, a:b])
+            elif kind == "ldr":
+                e, g0, g1, a, b = op[1:]
+                eng[e].dma_start(out=res[:, g0:g1, a:b], in_=r_rows[:, g0:g1, a:b])
+            elif kind == "cast":
+                e, key, a, b = op[1:]
+                home = [k for k in raw if k[0] == key and k[1] <= a and b <= k[2]][0]
+                piece = raw[home][:, :, a - home[1] : b - home[1]]
+                dst = grouped[key][:, a:b, :].rearrange("p (c i) t -> p c t i", i=4)
+                s = piece.rearrange("p t (c i) -> p c t i", i=4)
+                if e == "s":
+                    nc.scalar.copy(out=dst, in_=s)
+                elif e == "p":
+                    nc.gpsimd.tensor_scalar(out=dst, in0=s, scalar1=1.0, scalar2=0.0, op0=ALU.mult, op1=ALU.add)
+                else:
+                    nc.vector.tensor_copy(out=dst, in_=s)
+            elif kind == "q":
+                key, a, b = op[1:]
+                nc.vector.quantize_mx(
+                    out=codes[key][:, a:b].bitcast(FP8X4),
+                    scales=scales[key][:, a:b],
+                    in_=grouped[key][:, a:b, :].rearrange("p c t -> p (c t)"),
+                )
+            elif kind == "mm":
+                which, g, a = op[1:]
+                rows = slice(ROWS * g, ROWS * (g + 1))
+                nc.tensor.matmul_mx(
+                    out=banks[(g, which)][:, a : a + NT],
+                    lhsT=codes[which][rows, :].bitcast(FP8X4),
+                    lhsT_scale=scales[which][rows, :],
+                    rhs=codes["x"][rows, a : a + NT].bitcast(FP8X4),
+                    rhs_scale=scales["x"][rows, a : a + NT],
+                    start=True,
+                    stop=True,
+                )
+            elif kind == "sig":
+                g, a, b = op[1:]
+                nc.scalar.activation(out=gate[:, g, a:b], in_=banks[(g, "w")][:, a:b], func=ACT.Sigmoid)
+            elif kind == "mul":
+                g, a, b = op[1:]
+                nc.vector.tensor_tensor(out=prod[:, g, a:b], in0=banks[(g, "u")][:, a:b], in1=gate[:, g, a:b], op=ALU.mult)
+            elif kind == "add":
+                e, g0, g1, a, b = op[1:]
+                eng[e].tensor_tensor(out=y[:, g0:g1, a:b], in0=prod[:, g0:g1, a:b], in1=res[:, g0:g1, a:b], op=ALU.add)
+            elif kind == "st":
+                e, g0, g1, a, b = op[1:]
+                eng[e].dma_start(out=out_rows[:, g0:g1, a:b], in_=y[:, g0:g1, a:b])

@@ -20,101 +20,86 @@ NT = 128
 
 PROGRAM = [
     ("warm",),
+    ("ld", "y", "x", 0, 256),
     ("ld", "y", "w", 0, 128),
-    ("ld", "y", "x", 0, 128),
     ("ld", "y", "u", 0, 128),
-    ("ld", "y", "x", 128, 256),
-    ("ld", "y", "x", 256, 384),
-    ("ld", "y", "x", 384, 512),
-    ("ldr", "y", 0, 4, 0, 256),
-    ("ldr", "y", 0, 4, 256, 512),
-    ("cast", "s", "w", 0, 128),
-    ("cast", "v", "x", 0, 128),
+    ("ld", "y", "x", 256, 512),
+    ("ldr", "y", 0, 1, 0, 512),
+    ("ldr", "y", 1, 2, 0, 512),
+    ("ldr", "y", 2, 3, 0, 512),
+    ("ldr", "y", 3, 4, 0, 512),
+    ("cast", "v", "x", 0, 160),
+    ("cast", "s", "x", 160, 256),
+    ("cast", "v", "w", 0, 64),
+    ("cast", "s", "w", 64, 128),
+    ("q", "x", 0, 256),
     ("q", "w", 0, 128),
-    ("q", "x", 0, 128),
     ("mm", "w", 0, 0),
     ("mm", "w", 1, 0),
+    ("mm", "w", 0, 128),
+    ("mm", "w", 1, 128),
     ("mm", "w", 2, 0),
     ("mm", "w", 3, 0),
+    ("mm", "w", 2, 128),
+    ("mm", "w", 3, 128),
     ("cast", "v", "u", 0, 64),
     ("cast", "s", "u", 64, 128),
     ("q", "u", 0, 128),
     ("mm", "u", 0, 0),
     ("mm", "u", 1, 0),
+    ("mm", "u", 0, 128),
+    ("mm", "u", 1, 128),
     ("mm", "u", 2, 0),
     ("mm", "u", 3, 0),
-    ("cast", "v", "x", 128, 256),
-    ("q", "x", 128, 256),
-    ("sig", 0, 0, 128),
-    ("mm", "w", 0, 128),
-    ("sig", 1, 0, 128),
-    ("mm", "w", 1, 128),
-    ("sig", 2, 0, 128),
-    ("mm", "w", 2, 128),
-    ("sig", 3, 0, 128),
-    ("mm", "w", 3, 128),
-    ("mul", 0, 0, 128),
-    ("mm", "u", 0, 128),
-    ("mul", 1, 0, 128),
-    ("mm", "u", 1, 128),
-    ("mul", 2, 0, 128),
     ("mm", "u", 2, 128),
-    ("mul", 3, 0, 128),
     ("mm", "u", 3, 128),
-    ("cast", "s", "x", 256, 384),
-    ("q", "x", 256, 384),
-    ("sig", 0, 128, 256),
+    ("sig", 0, 0, 256),
+    ("cast", "v", "x", 256, 416),
+    ("cast", "s", "x", 416, 512),
+    ("mul", 0, 0, 256),
+    ("q", "x", 256, 512),
+    ("sig", 1, 0, 256),
+    ("sig", 2, 0, 256),
+    ("sig", 3, 0, 256),
     ("mm", "w", 0, 256),
-    ("sig", 1, 128, 256),
     ("mm", "w", 1, 256),
-    ("sig", 2, 128, 256),
-    ("mm", "w", 2, 256),
-    ("sig", 3, 128, 256),
-    ("mm", "w", 3, 256),
-    ("mul", 0, 128, 256),
-    ("mm", "u", 0, 256),
-    ("mul", 1, 128, 256),
-    ("mm", "u", 1, 256),
-    ("mul", 2, 128, 256),
-    ("mm", "u", 2, 256),
-    ("mul", 3, 128, 256),
-    ("mm", "u", 3, 256),
-    ("cast", "s", "x", 384, 512),
-    ("add", "v", 0, 1, 0, 256),
-    ("add", "v", 1, 2, 0, 256),
-    ("st", "y", 0, 2, 0, 256),
-    ("q", "x", 384, 512),
-    ("sig", 0, 256, 384),
     ("mm", "w", 0, 384),
-    ("sig", 1, 256, 384),
     ("mm", "w", 1, 384),
-    ("sig", 2, 256, 384),
-    ("mm", "w", 2, 384),
-    ("sig", 3, 256, 384),
-    ("mm", "w", 3, 384),
-    ("add", "v", 2, 3, 0, 256),
-    ("mul", 0, 256, 384),
+    ("add", "v", 0, 1, 0, 256),
+    ("st", "y", 0, 1, 0, 256),
+    ("mul", 1, 0, 256),
+    ("mm", "u", 0, 256),
+    ("mm", "u", 1, 256),
     ("mm", "u", 0, 384),
-    ("mul", 1, 256, 384),
     ("mm", "u", 1, 384),
-    ("mul", 2, 256, 384),
+    ("mul", 2, 0, 256),
+    ("add", "v", 1, 2, 0, 256),
+    ("st", "y", 1, 2, 0, 256),
+    ("mul", 3, 0, 256),
+    ("mm", "w", 2, 256),
+    ("mm", "w", 3, 256),
+    ("mm", "w", 2, 384),
+    ("mm", "w", 3, 384),
+    ("mm", "u", 2, 256),
+    ("mm", "u", 3, 256),
     ("mm", "u", 2, 384),
-    ("mul", 3, 256, 384),
     ("mm", "u", 3, 384),
+    ("sig", 0, 256, 512),
+    ("sig", 1, 256, 512),
+    ("sig", 2, 256, 512),
+    ("sig", 3, 256, 512),
+    ("add", "v", 2, 3, 0, 256),
+    ("st", "y", 2, 3, 0, 256),
+    ("mul", 0, 256, 512),
     ("add", "v", 3, 4, 0, 256),
-    ("st", "y", 2, 4, 0, 256),
-    ("sig", 0, 384, 512),
-    ("sig", 1, 384, 512),
-    ("sig", 2, 384, 512),
-    ("sig", 3, 384, 512),
-    ("mul", 0, 384, 512),
-    ("mul", 1, 384, 512),
+    ("st", "y", 3, 4, 0, 256),
+    ("mul", 1, 256, 512),
     ("add", "v", 0, 1, 256, 512),
     ("st", "y", 0, 1, 256, 512),
-    ("mul", 2, 384, 512),
+    ("mul", 2, 256, 512),
     ("add", "v", 1, 2, 256, 512),
     ("st", "y", 1, 2, 256, 512),
-    ("mul", 3, 384, 512),
+    ("mul", 3, 256, 512),
     ("add", "v", 2, 3, 256, 512),
     ("st", "y", 2, 3, 256, 512),
     ("add", "v", 3, 4, 256, 512),

@@ -38,10 +38,6 @@ PROGRAM = [
     ("mm", "w", 1, 0),
     ("mm", "w", 0, 128),
     ("mm", "w", 1, 128),
-    ("mm", "w", 2, 0),
-    ("mm", "w", 3, 0),
-    ("mm", "w", 2, 128),
-    ("mm", "w", 3, 128),
     ("cast", "v", "u", 0, 64),
     ("cast", "s", "u", 64, 128),
     ("q", "u", 0, 128),
@@ -49,13 +45,17 @@ PROGRAM = [
     ("mm", "u", 1, 0),
     ("mm", "u", 0, 128),
     ("mm", "u", 1, 128),
+    ("mm", "w", 2, 0),
+    ("mm", "w", 3, 0),
+    ("mm", "w", 2, 128),
+    ("mm", "w", 3, 128),
     ("mm", "u", 2, 0),
     ("mm", "u", 3, 0),
     ("mm", "u", 2, 128),
     ("mm", "u", 3, 128),
     ("sig", 0, 0, 256),
-    ("cast", "v", "x", 256, 416),
-    ("cast", "s", "x", 416, 512),
+    ("cast", "v", "x", 256, 400),
+    ("cast", "s", "x", 400, 512),
     ("mul", 0, 0, 256),
     ("q", "x", 256, 512),
     ("sig", 1, 0, 256),
@@ -65,7 +65,7 @@ PROGRAM = [
     ("mm", "w", 1, 256),
     ("mm", "w", 0, 384),
     ("mm", "w", 1, 384),
-    ("add", "v", 0, 1, 0, 256),
+    ("add", "p", 0, 1, 0, 256),
     ("st", "y", 0, 1, 0, 256),
     ("mul", 1, 0, 256),
     ("mm", "u", 0, 256),
@@ -73,8 +73,6 @@ PROGRAM = [
     ("mm", "u", 0, 384),
     ("mm", "u", 1, 384),
     ("mul", 2, 0, 256),
-    ("add", "v", 1, 2, 0, 256),
-    ("st", "y", 1, 2, 0, 256),
     ("mul", 3, 0, 256),
     ("mm", "w", 2, 256),
     ("mm", "w", 3, 256),
@@ -88,18 +86,20 @@ PROGRAM = [
     ("sig", 1, 256, 512),
     ("sig", 2, 256, 512),
     ("sig", 3, 256, 512),
+    ("add", "v", 1, 2, 0, 256),
+    ("st", "y", 1, 2, 0, 256),
     ("add", "v", 2, 3, 0, 256),
     ("st", "y", 2, 3, 0, 256),
-    ("mul", 0, 256, 512),
     ("add", "v", 3, 4, 0, 256),
     ("st", "y", 3, 4, 0, 256),
-    ("mul", 1, 256, 512),
-    ("add", "v", 0, 1, 256, 512),
+    ("mul", 0, 256, 512),
+    ("add", "p", 0, 1, 256, 512),
     ("st", "y", 0, 1, 256, 512),
+    ("mul", 1, 256, 512),
     ("mul", 2, 256, 512),
+    ("mul", 3, 256, 512),
     ("add", "v", 1, 2, 256, 512),
     ("st", "y", 1, 2, 256, 512),
-    ("mul", 3, 256, 512),
     ("add", "v", 2, 3, 256, 512),
     ("st", "y", 2, 3, 256, 512),
     ("add", "v", 3, 4, 256, 512),

@@ -15,185 +15,141 @@ ALU = mybir.AluOpType
 
 P = 128
 PACK = 4
-ROWS = 32
-NT = 128
+ROWS = D // PACK
+HALF = N // 2
+N_PASS = 128
+RUN = 4
 
-PROGRAM = [
-    ("warm",),
-    ("ld", "y", "x", 0, 256),
-    ("ld", "y", "w", 0, 128),
-    ("ld", "y", "u", 0, 128),
-    ("ld", "y", "x", 256, 512),
-    ("ldr", "y", 0, 1, 0, 512),
-    ("ldr", "y", 1, 2, 0, 512),
-    ("ldr", "y", 2, 3, 0, 512),
-    ("ldr", "y", 3, 4, 0, 512),
-    ("cast", "v", "x", 0, 160),
-    ("cast", "s", "x", 160, 256),
-    ("cast", "v", "w", 0, 64),
-    ("cast", "s", "w", 64, 128),
-    ("q", "x", 0, 256),
-    ("q", "w", 0, 128),
-    ("mm", "w", 0, 0),
-    ("mm", "w", 1, 0),
-    ("mm", "w", 0, 128),
-    ("mm", "w", 1, 128),
-    ("cast", "v", "u", 0, 64),
-    ("cast", "s", "u", 64, 128),
-    ("q", "u", 0, 128),
-    ("mm", "u", 0, 0),
-    ("mm", "u", 1, 0),
-    ("mm", "u", 0, 128),
-    ("mm", "u", 1, 128),
-    ("mm", "w", 2, 0),
-    ("mm", "w", 3, 0),
-    ("mm", "w", 2, 128),
-    ("mm", "w", 3, 128),
-    ("mm", "u", 2, 0),
-    ("mm", "u", 3, 0),
-    ("mm", "u", 2, 128),
-    ("mm", "u", 3, 128),
-    ("sig", 0, 0, 256),
-    ("cast", "v", "x", 256, 400),
-    ("cast", "s", "x", 400, 512),
-    ("mul", 0, 0, 256),
-    ("q", "x", 256, 512),
-    ("sig", 1, 0, 256),
-    ("sig", 2, 0, 256),
-    ("sig", 3, 0, 256),
-    ("mm", "w", 0, 256),
-    ("mm", "w", 1, 256),
-    ("mm", "w", 0, 384),
-    ("mm", "w", 1, 384),
-    ("add", "p", 0, 1, 0, 256),
-    ("st", "y", 0, 1, 0, 256),
-    ("mul", 1, 0, 256),
-    ("mm", "u", 0, 256),
-    ("mm", "u", 1, 256),
-    ("mm", "u", 0, 384),
-    ("mm", "u", 1, 384),
-    ("mul", 2, 0, 256),
-    ("mul", 3, 0, 256),
-    ("mm", "w", 2, 256),
-    ("mm", "w", 3, 256),
-    ("mm", "w", 2, 384),
-    ("mm", "w", 3, 384),
-    ("mm", "u", 2, 256),
-    ("mm", "u", 3, 256),
-    ("mm", "u", 2, 384),
-    ("mm", "u", 3, 384),
-    ("sig", 0, 256, 512),
-    ("sig", 1, 256, 512),
-    ("sig", 2, 256, 512),
-    ("sig", 3, 256, 512),
-    ("add", "v", 1, 2, 0, 256),
-    ("st", "y", 1, 2, 0, 256),
-    ("add", "v", 2, 3, 0, 256),
-    ("st", "y", 2, 3, 0, 256),
-    ("add", "v", 3, 4, 0, 256),
-    ("st", "y", 3, 4, 0, 256),
-    ("mul", 0, 256, 512),
-    ("add", "p", 0, 1, 256, 512),
-    ("st", "y", 0, 1, 256, 512),
-    ("mul", 1, 256, 512),
-    ("mul", 2, 256, 512),
-    ("mul", 3, 256, 512),
-    ("add", "v", 1, 2, 256, 512),
-    ("st", "y", 1, 2, 256, 512),
-    ("add", "v", 2, 3, 256, 512),
-    ("st", "y", 2, 3, 256, 512),
-    ("add", "v", 3, 4, 256, 512),
-    ("st", "y", 3, 4, 256, 512),
-]
+X_ON_VECTOR = 160
+W_ON_VECTOR = 64
 
 
 def tile_rows_gglu_sigmoid_res_kernel(tc, x, w, u, r, out):
     nc = tc.nc
-    src = {
-        "x": x.rearrange("g (p j) n -> (g p) j n", j=PACK),
-        "w": w.rearrange("g (p j) m -> (g p) j m", j=PACK),
-        "u": u.rearrange("g (p j) m -> (g p) j m", j=PACK),
-    }
+    x_rows = x.rearrange("g (p j) n -> (g p) j n", j=PACK)
+    w_rows = w.rearrange("g (p j) m -> (g p) j m", j=PACK)
+    u_rows = u.rearrange("g (p j) m -> (g p) j m", j=PACK)
     r_rows = r.rearrange("g m n -> m g n")
     out_rows = out.rearrange("g m n -> m g n")
-    eng = {"v": nc.vector, "s": nc.scalar, "p": nc.gpsimd, "y": nc.sync}
 
     with ExitStack() as ctx:
         sb = ctx.enter_context(tc.tile_pool(name="sb", bufs=1))
         ps = ctx.enter_context(tc.psum_pool(name="ps", bufs=1))
-        raw, grouped, codes, scales = {}, {}, {}, {}
-        for op in PROGRAM:
-            if op[0] == "ld":
-                raw[(op[2], op[3], op[4])] = sb.tile(
-                    [P, PACK, op[4] - op[3]], F32, name="raw_%s_%d" % (op[2], op[3]), align_bytes=64
-                )
-        for key, wd in (("w", M), ("u", M), ("x", N)):
-            grouped[key] = sb.tile([P, wd, PACK], BF16, name="grp_%s" % key, align_bytes=64)
-            codes[key] = sb.tile([P, wd], U32, name="codes_%s" % key, align_bytes=64)
-            scales[key] = sb.tile([P, wd], U8, name="scales_%s" % key, align_bytes=64)
+
+        x_raw = [sb.tile([P, PACK, HALF], F32, name="x_raw_%d" % h, align_bytes=64) for h in range(2)]
+        w_raw = sb.tile([P, PACK, M], F32, name="w_raw", align_bytes=64)
+        u_raw = sb.tile([P, PACK, M], F32, name="u_raw", align_bytes=64)
+
+        rounded, codes, scales = {}, {}, {}
+        for key, width in (("w", M), ("u", M), ("x", N)):
+            rounded[key] = sb.tile([P, width, PACK], BF16, name="rounded_" + key, align_bytes=64)
+            codes[key] = sb.tile([P, width], U32, name="codes_" + key, align_bytes=64)
+            scales[key] = sb.tile([P, width], U8, name="scales_" + key, align_bytes=64)
+
         banks = {}
         for g in range(G):
-            for which in ("w", "u"):
-                banks[(g, which)] = ps.tile([P, N], F32, name="bank_%d_%s" % (g, which))
+            for key in ("w", "u"):
+                banks[(g, key)] = ps.tile([P, N], F32, name="bank_%d_%s" % (g, key))
+
         gate = sb.tile([P, G, N], F32, name="gate", align_bytes=64)
-        prod = sb.tile([P, G, N], F32, name="prod", align_bytes=64)
-        res = sb.tile([P, G, N], F32, name="res", align_bytes=64)
-        y = sb.tile([P, G, N], F32, name="y", align_bytes=64)
-        warm = sb.tile([P, 8], F32, name="warm", align_bytes=64)
+        gated = sb.tile([P, G, N], F32, name="gated", align_bytes=64)
+        residual = sb.tile([P, G, N], F32, name="residual", align_bytes=64)
+        result = sb.tile([P, G, N], F32, name="result", align_bytes=64)
+        warm_in = sb.tile([P, 8], F32, name="warm_in", align_bytes=64)
         warm_out = sb.tile([P, 8], F32, name="warm_out", align_bytes=64)
 
+        def columns(h):
+            return slice(h * HALF, (h + 1) * HALF)
+
+        def round_to_bf16(raw, dst, on_vector):
+            width = raw.shape[2]
+            for a, b, copy in ((0, on_vector, nc.vector.tensor_copy), (on_vector, width, nc.scalar.copy)):
+                copy(
+                    out=dst[:, a:b, :].rearrange("p (c i) j -> p c j i", i=RUN),
+                    in_=raw[:, :, a:b].rearrange("p j (c i) -> p c j i", i=RUN),
+                )
+
+        def quantise(key, cols):
+            nc.vector.quantize_mx(
+                out=codes[key][:, cols].bitcast(FP8X4),
+                scales=scales[key][:, cols],
+                in_=rounded[key][:, cols, :].rearrange("p c j -> p (c j)"),
+            )
+
+        def products(h):
+            passes = [(key, h * HALF + n0) for key in ("w", "u") for n0 in range(0, HALF, N_PASS)]
+            for step in range(len(passes) + G - 1):
+                for g in range(G):
+                    if 0 <= step - g < len(passes):
+                        key, n0 = passes[step - g]
+                        rows = slice(ROWS * g, ROWS * (g + 1))
+                        cols = slice(n0, n0 + N_PASS)
+                        nc.tensor.matmul_mx(
+                            out=banks[(g, key)][:, cols],
+                            lhsT=codes[key][rows, :].bitcast(FP8X4),
+                            lhsT_scale=scales[key][rows, :],
+                            rhs=codes["x"][rows, cols].bitcast(FP8X4),
+                            rhs_scale=scales["x"][rows, cols],
+                            start=True,
+                            stop=True,
+                        )
+
+        def sigmoid(g, h):
+            nc.scalar.activation(out=gate[:, g, columns(h)], in_=banks[(g, "w")][:, columns(h)], func=ACT.Sigmoid)
+
+        def multiply(g, h):
+            nc.vector.tensor_tensor(
+                out=gated[:, g, columns(h)], in0=banks[(g, "u")][:, columns(h)], in1=gate[:, g, columns(h)], op=ALU.mult
+            )
+
+        def add_and_store(engine, first, last, h):
+            groups = slice(first, last + 1)
+            engine.tensor_tensor(
+                out=result[:, groups, columns(h)],
+                in0=gated[:, groups, columns(h)],
+                in1=residual[:, groups, columns(h)],
+                op=ALU.add,
+            )
+            nc.sync.dma_start(out=out_rows[:, groups, columns(h)], in_=result[:, groups, columns(h)])
+
         ctx.enter_context(tc.manual_schedule())
-        for op in PROGRAM:
-            kind = op[0]
-            if kind == "warm":
-                nc.gpsimd.memset(warm[:], 0.0)
-                nc.scalar.activation(out=warm_out[:], in_=warm[:], func=ACT.Sigmoid)
-            elif kind == "ld":
-                e, key, a, b = op[1:]
-                eng[e].dma_start(out=raw[(key, a, b)][:], in_=src[key][:, :, a:b])
-            elif kind == "ldr":
-                e, g0, g1, a, b = op[1:]
-                eng[e].dma_start(out=res[:, g0:g1, a:b], in_=r_rows[:, g0:g1, a:b])
-            elif kind == "cast":
-                e, key, a, b = op[1:]
-                home = [k for k in raw if k[0] == key and k[1] <= a and b <= k[2]][0]
-                piece = raw[home][:, :, a - home[1] : b - home[1]]
-                dst = grouped[key][:, a:b, :].rearrange("p (c i) t -> p c t i", i=4)
-                s = piece.rearrange("p t (c i) -> p c t i", i=4)
-                if e == "s":
-                    nc.scalar.copy(out=dst, in_=s)
-                elif e == "p":
-                    nc.gpsimd.tensor_scalar(out=dst, in0=s, scalar1=1.0, scalar2=0.0, op0=ALU.mult, op1=ALU.add)
-                else:
-                    nc.vector.tensor_copy(out=dst, in_=s)
-            elif kind == "q":
-                key, a, b = op[1:]
-                nc.vector.quantize_mx(
-                    out=codes[key][:, a:b].bitcast(FP8X4),
-                    scales=scales[key][:, a:b],
-                    in_=grouped[key][:, a:b, :].rearrange("p c t -> p (c t)"),
-                )
-            elif kind == "mm":
-                which, g, a = op[1:]
-                rows = slice(ROWS * g, ROWS * (g + 1))
-                nc.tensor.matmul_mx(
-                    out=banks[(g, which)][:, a : a + NT],
-                    lhsT=codes[which][rows, :].bitcast(FP8X4),
-                    lhsT_scale=scales[which][rows, :],
-                    rhs=codes["x"][rows, a : a + NT].bitcast(FP8X4),
-                    rhs_scale=scales["x"][rows, a : a + NT],
-                    start=True,
-                    stop=True,
-                )
-            elif kind == "sig":
-                g, a, b = op[1:]
-                nc.scalar.activation(out=gate[:, g, a:b], in_=banks[(g, "w")][:, a:b], func=ACT.Sigmoid)
-            elif kind == "mul":
-                g, a, b = op[1:]
-                nc.vector.tensor_tensor(out=prod[:, g, a:b], in0=banks[(g, "u")][:, a:b], in1=gate[:, g, a:b], op=ALU.mult)
-            elif kind == "add":
-                e, g0, g1, a, b = op[1:]
-                eng[e].tensor_tensor(out=y[:, g0:g1, a:b], in0=prod[:, g0:g1, a:b], in1=res[:, g0:g1, a:b], op=ALU.add)
-            elif kind == "st":
-                e, g0, g1, a, b = op[1:]
-                eng[e].dma_start(out=out_rows[:, g0:g1, a:b], in_=y[:, g0:g1, a:b])
+
+        nc.gpsimd.memset(warm_in[:], 0.0)
+        nc.scalar.activation(out=warm_out[:], in_=warm_in[:], func=ACT.Sigmoid)
+
+        nc.sync.dma_start(out=x_raw[0][:], in_=x_rows[:, :, columns(0)])
+        nc.sync.dma_start(out=w_raw[:], in_=w_rows)
+        nc.sync.dma_start(out=u_raw[:], in_=u_rows)
+        nc.sync.dma_start(out=x_raw[1][:], in_=x_rows[:, :, columns(1)])
+        for g in range(G):
+            nc.sync.dma_start(out=residual[:, g : g + 1, :], in_=r_rows[:, g : g + 1, :])
+
+        round_to_bf16(x_raw[0], rounded["x"][:, columns(0), :], X_ON_VECTOR)
+        round_to_bf16(w_raw, rounded["w"], W_ON_VECTOR)
+        quantise("x", columns(0))
+        quantise("w", slice(0, M))
+        round_to_bf16(u_raw, rounded["u"], W_ON_VECTOR)
+        quantise("u", slice(0, M))
+        products(0)
+
+        sigmoid(0, 0)
+        round_to_bf16(x_raw[1], rounded["x"][:, columns(1), :], X_ON_VECTOR)
+        multiply(0, 0)
+        quantise("x", columns(1))
+
+        for g in range(1, G):
+            sigmoid(g, 0)
+        add_and_store(nc.gpsimd, 0, 0, 0)
+        for g in range(1, G):
+            multiply(g, 0)
+        products(1)
+        for g in range(G):
+            sigmoid(g, 1)
+        add_and_store(nc.vector, 1, 2, 0)
+        multiply(0, 1)
+        add_and_store(nc.vector, 3, 3, 0)
+        add_and_store(nc.gpsimd, 0, 0, 1)
+        for g in range(1, G):
+            multiply(g, 1)
+        for g in range(1, G):
+            add_and_store(nc.vector, g, g, 1)

from contextlib import ExitStack

import concourse.mybir as mybir

G, D, M, N = 4, 128, 128, 512
FLOPS = 2 * 2 * G * D * M * N

F32 = mybir.dt.float32
BF16 = mybir.dt.bfloat16
U32 = mybir.dt.uint32
U8 = mybir.dt.uint8
FP8X4 = mybir.dt.float8_e4m3fn_x4
ACT = mybir.ActivationFunctionType
ALU = mybir.AluOpType

P = 128
PACK = 4
ROWS = D // PACK
HALF = N // 2
N_PASS = 128
RUN = 4

X_ON_VECTOR = 160
W_ON_VECTOR = 64


def tile_rows_gglu_sigmoid_res_kernel(tc, x, w, u, r, out):
    nc = tc.nc
    x_rows = x.rearrange("g (p j) n -> (g p) j n", j=PACK)
    w_rows = w.rearrange("g (p j) m -> (g p) j m", j=PACK)
    u_rows = u.rearrange("g (p j) m -> (g p) j m", j=PACK)
    r_rows = r.rearrange("g m n -> m g n")
    out_rows = out.rearrange("g m n -> m g n")

    with ExitStack() as ctx:
        sb = ctx.enter_context(tc.tile_pool(name="sb", bufs=1))
        ps = ctx.enter_context(tc.psum_pool(name="ps", bufs=1))

        x_raw = [sb.tile([P, PACK, HALF], F32, name="x_raw_%d" % h, align_bytes=64) for h in range(2)]
        w_raw = sb.tile([P, PACK, M], F32, name="w_raw", align_bytes=64)
        u_raw = sb.tile([P, PACK, M], F32, name="u_raw", align_bytes=64)

        rounded, codes, scales = {}, {}, {}
        for key, width in (("w", M), ("u", M), ("x", N)):
            rounded[key] = sb.tile([P, width, PACK], BF16, name="rounded_" + key, align_bytes=64)
            codes[key] = sb.tile([P, width], U32, name="codes_" + key, align_bytes=64)
            scales[key] = sb.tile([P, width], U8, name="scales_" + key, align_bytes=64)

        banks = {}
        for g in range(G):
            for key in ("w", "u"):
                banks[(g, key)] = ps.tile([P, N], F32, name="bank_%d_%s" % (g, key))

        gate = sb.tile([P, G, N], F32, name="gate", align_bytes=64)
        gated = sb.tile([P, G, N], F32, name="gated", align_bytes=64)
        residual = sb.tile([P, G, N], F32, name="residual", align_bytes=64)
        result = sb.tile([P, G, N], F32, name="result", align_bytes=64)
        warm_in = sb.tile([P, 8], F32, name="warm_in", align_bytes=64)
        warm_out = sb.tile([P, 8], F32, name="warm_out", align_bytes=64)

        def columns(h):
            return slice(h * HALF, (h + 1) * HALF)

        def round_to_bf16(raw, dst, on_vector):
            width = raw.shape[2]
            for a, b, copy in ((0, on_vector, nc.vector.tensor_copy), (on_vector, width, nc.scalar.copy)):
                copy(
                    out=dst[:, a:b, :].rearrange("p (c i) j -> p c j i", i=RUN),
                    in_=raw[:, :, a:b].rearrange("p j (c i) -> p c j i", i=RUN),
                )

        def quantise(key, cols):
            nc.vector.quantize_mx(
                out=codes[key][:, cols].bitcast(FP8X4),
                scales=scales[key][:, cols],
                in_=rounded[key][:, cols, :].rearrange("p c j -> p (c j)"),
            )

        def products(h):
            passes = [(key, h * HALF + n0) for key in ("w", "u") for n0 in range(0, HALF, N_PASS)]
            for step in range(len(passes) + G - 1):
                for g in range(G):
                    if 0 <= step - g < len(passes):
                        key, n0 = passes[step - g]
                        rows = slice(ROWS * g, ROWS * (g + 1))
                        cols = slice(n0, n0 + N_PASS)
                        nc.tensor.matmul_mx(
                            out=banks[(g, key)][:, cols],
                            lhsT=codes[key][rows, :].bitcast(FP8X4),
                            lhsT_scale=scales[key][rows, :],
                            rhs=codes["x"][rows, cols].bitcast(FP8X4),
                            rhs_scale=scales["x"][rows, cols],
                            start=True,
                            stop=True,
                        )

        def sigmoid(g, h):
            nc.scalar.activation(out=gate[:, g, columns(h)], in_=banks[(g, "w")][:, columns(h)], func=ACT.Sigmoid)

        def multiply(g, h):
            nc.vector.tensor_tensor(
                out=gated[:, g, columns(h)], in0=banks[(g, "u")][:, columns(h)], in1=gate[:, g, columns(h)], op=ALU.mult
            )

        def add_and_store(engine, first, last, h):
            groups = slice(first, last + 1)
            engine.tensor_tensor(
                out=result[:, groups, columns(h)],
                in0=gated[:, groups, columns(h)],
                in1=residual[:, groups, columns(h)],
                op=ALU.add,
            )
            nc.sync.dma_start(out=out_rows[:, groups, columns(h)], in_=result[:, groups, columns(h)])

        ctx.enter_context(tc.manual_schedule())

        nc.gpsimd.memset(warm_in[:], 0.0)
        nc.scalar.activation(out=warm_out[:], in_=warm_in[:], func=ACT.Sigmoid)

        nc.sync.dma_start(out=x_raw[0][:], in_=x_rows[:, :, columns(0)])
        nc.sync.dma_start(out=w_raw[:], in_=w_rows)
        nc.sync.dma_start(out=u_raw[:], in_=u_rows)
        nc.sync.dma_start(out=x_raw[1][:], in_=x_rows[:, :, columns(1)])
        for g in range(G):
            nc.sync.dma_start(out=residual[:, g : g + 1, :], in_=r_rows[:, g : g + 1, :])

        round_to_bf16(x_raw[0], rounded["x"][:, columns(0), :], X_ON_VECTOR)
        round_to_bf16(w_raw, rounded["w"], W_ON_VECTOR)
        quantise("x", columns(0))
        quantise("w", slice(0, M))
        round_to_bf16(u_raw, rounded["u"], W_ON_VECTOR)
        quantise("u", slice(0, M))
        products(0)

        sigmoid(0, 0)
        round_to_bf16(x_raw[1], rounded["x"][:, columns(1), :], X_ON_VECTOR)
        multiply(0, 0)
        quantise("x", columns(1))

        for g in range(1, G):
            sigmoid(g, 0)
        add_and_store(nc.gpsimd, 0, 0, 0)
        for g in range(1, G):
            multiply(g, 0)
        products(1)
        for g in range(G):
            sigmoid(g, 1)
        add_and_store(nc.vector, 1, 2, 0)
        multiply(0, 1)
        add_and_store(nc.vector, 3, 3, 0)
        add_and_store(nc.gpsimd, 0, 0, 1)
        for g in range(1, G):
            multiply(g, 1)
        for g in range(1, G):
            add_and_store(nc.vector, g, g, 1)
